import numpy as np
import ml_dtypes


def mxq(x, axis, fmt="e4m3"):
    dtype, down = {"e4m3": (ml_dtypes.float8_e4m3fn, 7), "e5m2": (ml_dtypes.float8_e5m2, 14)}[fmt]
    v = np.moveaxis(np.asarray(x, np.float32).astype(ml_dtypes.bfloat16).astype(np.float64), axis, -1)
    blocks = v.reshape(v.shape[:-1] + (-1, 32))
    amax = np.abs(blocks).max(-1, keepdims=True)
    byte = np.maximum(np.where(amax > 0, np.frexp(amax)[1] - 1 + 127, 0) - down, 1)
    scale = np.exp2(byte - 127.0)
    codes = (blocks / scale).astype(np.float32).astype(dtype).astype(np.float64)
    return np.moveaxis((codes * scale).reshape(v.shape), -1, axis)


WIDE = False


def mx_kscale(k):
    if not WIDE:
        return np.ones(k)
    levels = np.array([10, -10, 5, -5, 0])
    if k % 512:
        return np.exp2(np.random.permutation(np.resize(levels, k // 32))).repeat(32)
    a = np.empty((k // 512, 16))
    for p in range(k // 512):
        a[p, :8] = np.random.permutation(np.resize(levels, 8))
        for g in range(8):
            far = levels[np.abs(levels - a[p, g]) >= 10]
            a[p, g + 8] = far[np.random.randint(len(far))]
    return np.exp2(a.ravel()).repeat(32)


def f64(x):
    return np.asarray(x).astype(np.float64)


def striped(idx):
    return np.tile(np.asarray(idx).reshape(-1, 16).T, (8, 1)).astype(np.uint16)


def unstriped(offs):
    return offs[:16].T.reshape(-1).astype(np.int64)


E2M1 = np.array([0.0, 0.5, 1.0, 1.5, 2.0, 3.0, 4.0, 6.0, -0.0, -0.5, -1.0, -1.5, -2.0, -3.0, -4.0, -6.0])


def pack_weight(w, fmt):
    k, n = w.shape
    w = f64(np.asarray(w, np.float32).astype(ml_dtypes.bfloat16)).reshape(k // 32, 32, n)
    amax = np.abs(w).max(1)
    if fmt == "e4m3":
        byte = np.frexp(amax)[1] - 1 + 127 - 7
    else:
        mant, ex = np.frexp(amax / 6.0)
        byte = np.where(mant > 0.5, ex, ex - 1) + 127
    byte = np.clip(np.where(amax > 0, byte, 1), 1, 254)
    scaled = (w * np.exp2(127.0 - byte)[:, None, :]).reshape(k, n).astype(np.float32)
    by_word = np.ascontiguousarray(scaled.reshape(k // 512, 128, 4, n).transpose(0, 1, 3, 2))
    if fmt == "e4m3":
        words = by_word.astype(ml_dtypes.float8_e4m3fn).view(np.uint8)
    else:
        c = by_word.astype(ml_dtypes.float4_e2m1fn).view(np.uint8) & 0xF
        words = (c[..., 0::2] | (c[..., 1::2] << 4)).reshape(k // 512, 128, 2 * n)
    return np.ascontiguousarray(words), np.ascontiguousarray(byte.astype(np.uint8).reshape(k // 512, 16, n))


def unpack_weight(words, scales, fmt):
    g, _, n = scales.shape
    words = np.ascontiguousarray(words).reshape(g, 128, n, -1)
    if fmt == "e4m3":
        vals = words.view(ml_dtypes.float8_e4m3fn).astype(np.float64)
    else:
        nib = np.empty((g, 128, n, 4), np.uint8)
        nib[..., 0::2] = words & 0xF
        nib[..., 1::2] = words >> 4
        vals = E2M1[nib]
    vals = vals * np.repeat(np.exp2(scales.astype(np.float64) - 127.0), 8, axis=1)[..., None]
    return vals.transpose(0, 1, 3, 2).reshape(g * 512, n)


def bf(x):
    return np.asarray(x, np.float32).astype(ml_dtypes.bfloat16)


def planes(Y):
    r, m = Y.shape
    b = f64(bf(Y)).reshape(r // 32, 32, m)
    amax = np.abs(b).max(1)
    byte = np.clip(np.where(amax > 0, np.frexp(amax)[1] - 1 + 127 - 7, 1), 1, 254)
    codes = (b * np.exp2(127.0 - byte)[:, None, :]).reshape(r, m).astype(np.float32).astype(ml_dtypes.float8_e4m3fn).view(np.uint8)
    words = codes.reshape(r // 512, 128, 4, m).transpose(0, 1, 3, 2)
    return np.ascontiguousarray(words), np.ascontiguousarray(byte.astype(np.uint8).reshape(r // 512, 16, m))


D, T, I, Q, E = 512, 2048, 512, 256, 512


def setup_inputs():
    n = np.random.standard_normal
    idx = np.random.permutation(T)[:I]
    idx2 = np.random.permutation(T)[:I]
    idx3 = np.random.permutation(T)[:I]
    fd = mx_kscale(D)
    fi = mx_kscale(I)
    ti = np.ones(T)
    ti[idx] = fi
    keysp = pack_weight(n((D, T)) / fd[:, None], "e2m1")
    return {
        "query": (n((D, Q)) * 0.78 / np.sqrt(D) * fd[:, None]).astype(np.float32),
        "keys_words": keysp[0],
        "keys_scales": keysp[1],
        "lam": (np.random.uniform(0.8, 1.8, (Q, 1))).astype(np.float32),
        "level": (np.random.uniform(0.05, 0.2, (Q, 1))).astype(np.float32),
        "os": (np.random.uniform(4.0, 16.0, (1, I)) * fi).astype(np.float32),
        "vals": (n((E, T)) / ti).astype(np.float32),
        "before": (n((E, Q))).astype(np.float32),
        "hold": (np.random.uniform(0.1, 0.6, (1, Q))).astype(np.float32),
        "offs": striped(idx),
        "offs2": striped(idx2),
        "offs3": striped(idx3),
    }


def reference(query, keys_words, keys_scales, lam, level, os, vals, before, hold, offs, offs2, offs3):
    idx = unstriped(offs)
    idx2 = unstriped(offs2)
    idx3 = unstriped(offs3)
    keysu = unpack_weight(keys_words, keys_scales, "e2m1")
    queryq = mxq(f64(query), 0, "e4m3")
    a = queryq.T @ keysu
    lo2 = np.minimum(a[:, idx], a[:, idx2])
    hi2 = np.maximum(a[:, idx], a[:, idx2])
    s = np.maximum(lo2, np.minimum(hi2, a[:, idx3])) * f64(lam)
    p = np.exp(s - np.max(s, axis=1, keepdims=True))
    r = p / np.sum(p, axis=1, keepdims=True)
    w = np.maximum(r - np.max(r, axis=1, keepdims=True) * f64(level), 0.0)
    wo1 = w * f64(os)
    wt1 = wo1.T
    vt1 = f64(vals)[:, idx].T
    vt1q = mxq(vt1, 0, "e4m3")
    wt1q = mxq(wt1, 0, "e4m3")
    o = vt1q.T @ wt1q
    y = f64(before) * f64(hold) + o * (1.0 - f64(hold))
    words, scales = planes(y)
    return y, words, scales

@@ -1,0 +1,263 @@
+from contextlib import ExitStack
+
+import concourse.mybir as mybir
+from concourse.masks import make_identity
+
+D, T, I, Q, E = 512, 2048, 512, 256, 512
+FLOPS = 2 * D * Q * T + 2 * I * E * Q
+
+F32 = mybir.dt.float32
+BF16 = mybir.dt.bfloat16
+I32 = mybir.dt.int32
+U32 = mybir.dt.uint32
+U16 = mybir.dt.uint16
+U8 = mybir.dt.uint8
+FP8X4 = mybir.dt.float8_e4m3fn_x4
+FP4X4 = mybir.dt.float4_e2m1fn_x4
+ALU = mybir.AluOpType
+ACT = mybir.ActivationFunctionType
+
+P = 128
+PACK = 4
+BANK = 512
+QT = Q // P
+
+
+def tile_attend_middle_excess_blend_pl_kernel(
+    tc, query, keys_words, keys_scales, lam, level, slot_factor, vals, before, hold, offs, offs2, offs3,
+    out_0, out_1, out_2,
+):
+    nc = tc.nc
+    with ExitStack() as ctx:
+        sb = ctx.enter_context(tc.tile_pool(name="sb", bufs=1))
+        ps = ctx.enter_context(tc.psum_pool(name="ps", bufs=1))
+
+        def bank(b, name):
+            return ps.tile([P, BANK], F32, name=name, tag="bank%d" % b)
+
+        key_scales = sb.tile([P, T], U8, name="key_scales", align_bytes=64)
+        nc.vector.memset(key_scales[:].bitcast(I32), 0)
+
+        query_rows = query.rearrange("(p t) q -> p t q", t=PACK)
+        q_raw = [sb.tile([P, PACK, P], F32, name="q_raw%d" % h) for h in range(QT)]
+        key_words = [sb.tile([P, T], U8, name="key_words%d" % c, align_bytes=64) for c in range(2)]
+        nc.sync.dma_start(out=q_raw[0][:], in_=query_rows[:, :, 0:P])
+        for quad in range(4):
+            nc.sync.dma_start(
+                out=key_scales[32 * quad : 32 * quad + 4, :].bitcast(I32),
+                in_=keys_scales[0, 4 * quad : 4 * quad + 4, :].bitcast(I32),
+            )
+        for c in range(2):
+            nc.sync.dma_start(
+                out=key_words[c][:].bitcast(I32), in_=keys_words[0, :, c * T : (c + 1) * T].bitcast(I32)
+            )
+        nc.sync.dma_start(out=q_raw[1][:], in_=query_rows[:, :, P : 2 * P])
+        before_sb = sb.tile([P, PACK, Q], F32, name="before_sb")
+        lists = [sb.tile([P, I // 16], U16, name="list%d" % k) for k in range(3)]
+        vals_rows = vals.rearrange("(p j) t -> j p t", j=PACK)
+        vals_sb = [sb.tile([P, T], F32, name="vals_sb%d" % j) for j in range(PACK)]
+        factor_col = sb.tile([P, PACK], F32, name="factor_col")
+        ident = sb.tile([P, P], F32, name="ident")
+        rows = sb.tile([P, P], F32, name="rows")
+        nc.gpsimd.memset(rows[:], 0.0)
+        nc.sync.dma_start(out=before_sb[:], in_=before.rearrange("(p j) q -> p j q", j=PACK))
+        nc.sync.dma_start(out=rows[0:QT, :], in_=hold.rearrange("o (h p) -> (o h) p", p=P))
+        for k, src in enumerate((offs, offs2, offs3)):
+            nc.sync.dma_start(lists[k][:], src)
+        nc.sync.dma_start(out=rows[QT : 2 * QT, :], in_=lam.rearrange("(h p) o -> h (p o)", p=P))
+        nc.sync.dma_start(out=rows[2 * QT : 3 * QT, :], in_=level.rearrange("(h p) o -> h (p o)", p=P))
+        nc.sync.dma_start(out=vals_sb[0][:], in_=vals_rows[0])
+        nc.sync.dma_start(out=vals_sb[1][:], in_=vals_rows[1])
+        nc.sync.dma_start(out=factor_col[:], in_=slot_factor.rearrange("o (p t) -> p (o t)", t=PACK))
+        for j in range(2, PACK):
+            nc.sync.dma_start(out=vals_sb[j][:], in_=vals_rows[j])
+        make_identity(nc, ident[:])
+
+        q_bf = [sb.tile([P, P, PACK], BF16, name="q_bf%d" % h, align_bytes=64) for h in range(QT)]
+        q_codes = [sb.tile([P, P], U32, name="q_codes%d" % h, align_bytes=64) for h in range(QT)]
+        q_scales = [sb.tile([P, P], U8, name="q_scales%d" % h, align_bytes=64) for h in range(QT)]
+        a_sb = [sb.tile([P, T], F32, name="a_sb%d" % h) for h in range(QT)]
+        score_banks = [[0, 1, 2, 3], [4, 5, 0, 1]]
+        for h in range(QT):
+            nc.vector.tensor_copy(out=q_bf[h][:], in_=q_raw[h][:].rearrange("p t q -> p q t"))
+            nc.vector.quantize_mx(
+                out=q_codes[h][:].bitcast(FP8X4), scales=q_scales[h][:], in_=q_bf[h][:].rearrange("p q t -> p (q t)")
+            )
+        for h in range(QT):
+            for c in range(T // BANK):
+                acc = bank(score_banks[h][c], "score%d_%d" % (h, c))
+                half, rest = divmod(c, 2)
+                nc.tensor.matmul_mx(
+                    out=acc[:],
+                    lhsT=q_codes[h][:].bitcast(FP8X4),
+                    lhsT_scale=q_scales[h][:],
+                    rhs=key_words[half][:, rest * 2 * BANK : (rest + 1) * 2 * BANK].bitcast(FP4X4),
+                    rhs_scale=key_scales[:, c * BANK : (c + 1) * BANK],
+                    start=True,
+                    stop=True,
+                )
+                dst = a_sb[h][:, c * BANK : (c + 1) * BANK]
+                if h == 0 and c % 2 == 1:
+                    nc.vector.tensor_copy(out=dst, in_=acc[:])
+                else:
+                    nc.scalar.copy(out=dst, in_=acc[:])
+
+        rows_turned = bank(7, "rows_turned")
+        nc.tensor.transpose(rows_turned[:, 0:P], rows[:], ident[:])
+        cols_sb = sb.tile([P, 3 * QT], F32, name="cols_sb")
+        nc.vector.tensor_copy(out=cols_sb[:], in_=rows_turned[:, 0 : 3 * QT])
+        hold_col = cols_sb[:, 0:QT]
+        lam_col = cols_sb[:, QT : 2 * QT]
+        level_col = cols_sb[:, 2 * QT : 3 * QT]
+
+        hold_ps = bank(6, "hold_ps")
+        for h in range(QT):
+            nc.tensor.transpose(hold_ps[:, h * P : (h + 1) * P], hold_col[:, h : h + 1].to_broadcast([P, P]), ident[:])
+        kept = sb.tile([P, PACK, Q], F32, name="kept")
+        nc.vector.tensor_tensor(
+            out=kept[:], in0=before_sb[:], in1=hold_ps[:, 0:Q].unsqueeze(1).to_broadcast([P, PACK, Q]), op=ALU.mult
+        )
+        rest_row = sb.tile([P, Q], F32, name="rest_row")
+        nc.vector.tensor_scalar(rest_row[:], hold_ps[:, 0:Q], -1.0, 1.0, op0=ALU.mult, op1=ALU.add)
+        neg_lam = sb.tile([P, QT], F32, name="neg_lam")
+        nc.vector.tensor_scalar(neg_lam[:], lam_col, -1.0, None, op0=ALU.mult)
+
+        def gather(on_vector, dst, window, k):
+            if on_vector:
+                nc.vector.tensor_copy(dst, window.indirect(lists[k][:]))
+            else:
+                nc.scalar.activation(dst, window.indirect(lists[k][:]), ACT.Copy)
+
+        picked = [[sb.tile([P, I], F32, name="picked%d_%d" % (h, k)) for k in range(3)] for h in range(QT)]
+        neg_s = [sb.tile([P, I], F32, name="neg_s%d" % h) for h in range(QT)]
+        neg_max = [sb.tile([P, 1], F32, name="neg_max%d" % h) for h in range(QT)]
+        expd = [sb.tile([P, PACK, P], F32, name="expd%d" % h) for h in range(QT)]
+        total = [sb.tile([P, 1], F32, name="total%d" % h) for h in range(QT)]
+        inv_total = [sb.tile([P, 1], F32, name="inv_total%d" % h) for h in range(QT)]
+        excess = [sb.tile([P, PACK, P], F32, name="excess%d" % h) for h in range(QT)]
+        w_bf = [sb.tile([P, P, PACK], BF16, name="w_bf%d" % h, align_bytes=64) for h in range(QT)]
+        w_codes = [sb.tile([P, P], U32, name="w_codes%d" % h, align_bytes=64) for h in range(QT)]
+        w_scales = [sb.tile([P, P], U8, name="w_scales%d" % h, align_bytes=64) for h in range(QT)]
+
+        def median(h):
+            x, y, z = picked[h]
+            lo = sb.tile([P, I], F32, name="lo%d" % h)
+            hi = sb.tile([P, I], F32, name="hi%d" % h)
+            nc.vector.tensor_tensor(out=hi[:], in0=x[:], in1=y[:], op=ALU.max)
+            nc.vector.tensor_tensor(out=lo[:], in0=x[:], in1=y[:], op=ALU.min)
+            nc.vector.tensor_tensor(out=hi[:], in0=hi[:], in1=z[:], op=ALU.min)
+            nc.vector.tensor_tensor(out=lo[:], in0=lo[:], in1=hi[:], op=ALU.max)
+            nc.vector.tensor_scalar(
+                neg_s[h][:], lo[:], neg_lam[:, h : h + 1], None, op0=ALU.mult, op1=ALU.min, accum_out=neg_max[h][:]
+            )
+
+        def exponent(h):
+            nc.scalar.activation(
+                out=expd[h][:].rearrange("p t s -> p s t"),
+                in_=neg_s[h][:].rearrange("p (s t) -> p s t", t=PACK),
+                func=ACT.Exp,
+                bias=neg_max[h][:],
+                scale=-1.0,
+                accum_out=total[h][:],
+            )
+
+        def weights(h):
+            nc.vector.reciprocal(inv_total[h][:], total[h][:])
+            nc.vector.tensor_scalar(
+                excess[h][:], expd[h][:], level_col[:, h : h + 1], inv_total[h][:], op0=ALU.subtract, op1=ALU.mult
+            )
+            turned = bank(2 + h, "w_turned%d" % h)
+            for t in range(PACK):
+                nc.tensor.transpose(turned[:, t * P : (t + 1) * P], excess[h][:, t, :], ident[:])
+            nc.vector.scalar_tensor_tensor(
+                out=w_bf[h][:],
+                in0=turned[:].rearrange("p (t q) -> p q t", t=PACK),
+                scalar=0.0,
+                in1=factor_col[:].unsqueeze(1).to_broadcast([P, P, PACK]),
+                op0=ALU.max,
+                op1=ALU.mult,
+            )
+            nc.vector.quantize_mx(
+                out=w_codes[h][:].bitcast(FP8X4), scales=w_scales[h][:], in_=w_bf[h][:].rearrange("p q t -> p (q t)")
+            )
+
+        v_picked = [sb.tile([P, I], BF16, name="v_picked%d" % j) for j in range(PACK)]
+        v_bf = [sb.tile([P, 2 * P * PACK], BF16, name="v_bf%d" % g, align_bytes=64) for g in range(2)]
+        v_codes = [sb.tile([P, 2 * P], U32, name="v_codes%d" % g, align_bytes=64) for g in range(2)]
+        v_scales = [sb.tile([P, 2 * P], U8, name="v_scales%d" % g, align_bytes=64) for g in range(2)]
+
+        def values(g):
+            turned = bank(6 + (g + 1) % 2, "v_turned%d" % g)
+            for jj in range(2):
+                j = 2 * g + jj
+                gather(j in (0, 3), v_picked[j][:], vals_sb[j][:], 0)
+                words = v_picked[j][:].bitcast(F32)
+                for u in range(2):
+                    col = (2 * jj + u) * P
+                    nc.tensor.transpose(turned[:, col : col + P], words[:, u : I // 2 : 2], ident[:])
+            nc.scalar.copy(
+                out=v_bf[g][:].bitcast(F32).rearrange("p (j e u) -> p j e u", j=2, u=2),
+                in_=turned[:].rearrange("p (j u e) -> p j e u", j=2, u=2),
+            )
+            nc.vector.quantize_mx(out=v_codes[g][:].bitcast(FP8X4), scales=v_scales[g][:], in_=v_bf[g][:])
+
+        y_sb = [sb.tile([P, PACK, P], F32, name="y_sb%d" % h) for h in range(QT)]
+        y_bf = [sb.tile([P, P, PACK], BF16, name="y_bf%d" % h, align_bytes=64) for h in range(QT)]
+        y_codes = [sb.tile([P, P], U32, name="y_codes%d" % h, align_bytes=64) for h in range(QT)]
+        y_scales = sb.tile([P, Q], U8, name="y_scales", align_bytes=64)
+        out_rows = out_0.rearrange("(p j) q -> p j q", j=PACK)
+        out_words = out_1[0].rearrange("p q t -> p (q t)").bitcast(I32)
+
+        def blend(h):
+            cols = slice(h * P, (h + 1) * P)
+            acc = bank(4 + h, "o%d" % h)
+            for j in range(PACK):
+                g, jj = divmod(j, 2)
+                nc.tensor.matmul_mx(
+                    out=acc[:, j * P : (j + 1) * P],
+                    lhsT=v_codes[g][:, jj * P : (jj + 1) * P].bitcast(FP8X4),
+                    lhsT_scale=v_scales[g][:, jj * P : (jj + 1) * P],
+                    rhs=w_codes[h][:].bitcast(FP8X4),
+                    rhs_scale=w_scales[h][:],
+                    start=True,
+                    stop=True,
+                )
+            fresh = sb.tile([P, PACK, P], F32, name="fresh%d" % h)
+            nc.vector.tensor_tensor(
+                out=fresh[:],
+                in0=acc[:].rearrange("p (j q) -> p j q", j=PACK),
+                in1=rest_row[:, cols].unsqueeze(1).to_broadcast([P, PACK, P]),
+                op=ALU.mult,
+            )
+            nc.vector.tensor_tensor(out=y_sb[h][:], in0=fresh[:], in1=kept[:, :, cols], op=ALU.add)
+            nc.sync.dma_start(out=out_rows[:, :, cols], in_=y_sb[h][:])
+            if h == 0:
+                nc.scalar.copy(out=y_bf[h][:], in_=y_sb[h][:].rearrange("p j q -> p q j"))
+            else:
+                nc.vector.tensor_copy(out=y_bf[h][:], in_=y_sb[h][:].rearrange("p j q -> p q j"))
+            nc.vector.quantize_mx(
+                out=y_codes[h][:].bitcast(FP8X4), scales=y_scales[:, cols], in_=y_bf[h][:].rearrange("p q t -> p (q t)")
+            )
+            nc.sync.dma_start(out=out_words[:, cols], in_=y_codes[h][:].bitcast(I32))
+
+        gather(True, picked[0][0][:], a_sb[0][:], 0)
+        gather(False, picked[0][2][:], a_sb[0][:], 2)
+        gather(True, picked[0][1][:], a_sb[0][:], 1)
+        median(0)
+        for k in range(3):
+            gather(False, picked[1][k][:], a_sb[1][:], k)
+        exponent(0)
+        median(1)
+        weights(0)
+        values(0)
+        exponent(1)
+        values(1)
+        weights(1)
+        blend(0)
+        blend(1)
+        for quad in range(4):
+            queue = nc.scalar if quad % 2 else nc.sync
+            queue.dma_start(
+                out=out_2[0, 4 * quad : 4 * quad + 4, :].bitcast(I32),
+                in_=y_scales[32 * quad : 32 * quad + 4, :].bitcast(I32),
+            )

@@ -41,36 +41,43 @@ def tile_attend_middle_excess_blend_pl_kernel(
         query_rows = query.rearrange("(p t) q -> p t q", t=PACK)
         q_raw = [sb.tile([P, PACK, P], F32, name="q_raw%d" % h) for h in range(QT)]
         key_words = [sb.tile([P, T], U8, name="key_words%d" % c, align_bytes=64) for c in range(2)]
-        nc.sync.dma_start(out=q_raw[0][:], in_=query_rows[:, :, 0:P])
-        for quad in range(4):
-            nc.sync.dma_start(
-                out=key_scales[32 * quad : 32 * quad + 4, :].bitcast(I32),
-                in_=keys_scales[0, 4 * quad : 4 * quad + 4, :].bitcast(I32),
-            )
-        for c in range(2):
-            nc.sync.dma_start(
-                out=key_words[c][:].bitcast(I32), in_=keys_words[0, :, c * T : (c + 1) * T].bitcast(I32)
-            )
-        nc.sync.dma_start(out=q_raw[1][:], in_=query_rows[:, :, P : 2 * P])
         before_sb = sb.tile([P, PACK, Q], F32, name="before_sb")
         lists = [sb.tile([P, I // 16], U16, name="list%d" % k) for k in range(3)]
         vals_rows = vals.rearrange("(p j) t -> j p t", j=PACK)
         vals_sb = [sb.tile([P, T], F32, name="vals_sb%d" % j) for j in range(PACK)]
         factor_col = sb.tile([P, PACK], F32, name="factor_col")
+        hold_col = sb.tile([P, QT], F32, name="hold_col")
+        lam_col = sb.tile([P, QT], F32, name="lam_col")
+        level_col = sb.tile([P, QT], F32, name="level_col")
         ident = sb.tile([P, P], F32, name="ident")
-        rows = sb.tile([P, P], F32, name="rows")
-        nc.gpsimd.memset(rows[:], 0.0)
-        nc.sync.dma_start(out=before_sb[:], in_=before.rearrange("(p j) q -> p j q", j=PACK))
-        nc.sync.dma_start(out=rows[0:QT, :], in_=hold.rearrange("o (h p) -> (o h) p", p=P))
+
+        def load_keys(c):
+            nc.sync.dma_start(
+                out=key_words[c][:].bitcast(I32), in_=keys_words[0, :, c * T : (c + 1) * T].bitcast(I32)
+            )
+
+        def load_columns(dst, src):
+            with nc.allow_non_contiguous_dma(reason="one value a partition"):
+                nc.sync.dma_start(out=dst, in_=src)
+
+        nc.sync.dma_start(out=q_raw[0][:], in_=query_rows[:, :, 0:P])
+        load_keys(0)
+        for quad in range(4):
+            nc.sync.dma_start(
+                out=key_scales[32 * quad : 32 * quad + 4, :].bitcast(I32),
+                in_=keys_scales[0, 4 * quad : 4 * quad + 4, :].bitcast(I32),
+            )
+        nc.sync.dma_start(out=q_raw[1][:], in_=query_rows[:, :, P : 2 * P])
+        load_keys(1)
         for k, src in enumerate((offs, offs2, offs3)):
             nc.sync.dma_start(lists[k][:], src)
-        nc.sync.dma_start(out=rows[QT : 2 * QT, :], in_=lam.rearrange("(h p) o -> h (p o)", p=P))
-        nc.sync.dma_start(out=rows[2 * QT : 3 * QT, :], in_=level.rearrange("(h p) o -> h (p o)", p=P))
-        nc.sync.dma_start(out=vals_sb[0][:], in_=vals_rows[0])
-        nc.sync.dma_start(out=vals_sb[1][:], in_=vals_rows[1])
-        nc.sync.dma_start(out=factor_col[:], in_=slot_factor.rearrange("o (p t) -> p (o t)", t=PACK))
-        for j in range(2, PACK):
+        load_columns(hold_col[:], hold.rearrange("o (h p) -> p (o h)", p=P))
+        nc.sync.dma_start(out=before_sb[:], in_=before.rearrange("(p j) q -> p j q", j=PACK))
+        for j in range(PACK):
             nc.sync.dma_start(out=vals_sb[j][:], in_=vals_rows[j])
+        load_columns(lam_col[:], lam.rearrange("(h p) o -> p (h o)", p=P))
+        load_columns(level_col[:], level.rearrange("(h p) o -> p (h o)", p=P))
+        nc.sync.dma_start(out=factor_col[:], in_=slot_factor.rearrange("o (p t) -> p (o t)", t=PACK))
         make_identity(nc, ident[:])
 
         q_bf = [sb.tile([P, P, PACK], BF16, name="q_bf%d" % h, align_bytes=64) for h in range(QT)]
@@ -97,30 +104,18 @@ def tile_attend_middle_excess_blend_pl_kernel(
                     stop=True,
                 )
                 dst = a_sb[h][:, c * BANK : (c + 1) * BANK]
-                if h == 0 and c % 2 == 1:
+                if c % 2 == 1:
                     nc.vector.tensor_copy(out=dst, in_=acc[:])
                 else:
                     nc.scalar.copy(out=dst, in_=acc[:])
 
-        rows_turned = bank(7, "rows_turned")
-        nc.tensor.transpose(rows_turned[:, 0:P], rows[:], ident[:])
-        cols_sb = sb.tile([P, 3 * QT], F32, name="cols_sb")
-        nc.vector.tensor_copy(out=cols_sb[:], in_=rows_turned[:, 0 : 3 * QT])
-        hold_col = cols_sb[:, 0:QT]
-        lam_col = cols_sb[:, QT : 2 * QT]
-        level_col = cols_sb[:, 2 * QT : 3 * QT]
-
-        hold_ps = bank(6, "hold_ps")
+        hold_ps = bank(0, "hold_ps")
         for h in range(QT):
             nc.tensor.transpose(hold_ps[:, h * P : (h + 1) * P], hold_col[:, h : h + 1].to_broadcast([P, P]), ident[:])
-        kept = sb.tile([P, PACK, Q], F32, name="kept")
-        nc.vector.tensor_tensor(
-            out=kept[:], in0=before_sb[:], in1=hold_ps[:, 0:Q].unsqueeze(1).to_broadcast([P, PACK, Q]), op=ALU.mult
-        )
         rest_row = sb.tile([P, Q], F32, name="rest_row")
-        nc.vector.tensor_scalar(rest_row[:], hold_ps[:, 0:Q], -1.0, 1.0, op0=ALU.mult, op1=ALU.add)
+        nc.scalar.activation(out=rest_row[:], in_=hold_ps[:, 0:Q], func=ACT.Copy, scale=-1.0, bias=1.0)
         neg_lam = sb.tile([P, QT], F32, name="neg_lam")
-        nc.vector.tensor_scalar(neg_lam[:], lam_col, -1.0, None, op0=ALU.mult)
+        nc.gpsimd.tensor_scalar(neg_lam[:], lam_col[:], -1.0, 0.0, op0=ALU.mult, op1=ALU.add)
 
         def gather(on_vector, dst, window, k):
             if on_vector:
@@ -129,19 +124,19 @@ def tile_attend_middle_excess_blend_pl_kernel(
                 nc.scalar.activation(dst, window.indirect(lists[k][:]), ACT.Copy)
 
         picked = [[sb.tile([P, I], F32, name="picked%d_%d" % (h, k)) for k in range(3)] for h in range(QT)]
-        neg_s = [sb.tile([P, I], F32, name="neg_s%d" % h) for h in range(QT)]
+        neg_s = [sb.tile([P, I], F32, name="neg_s%d" % h, tag="neg_s%d" % h, align_bytes=64) for h in range(QT)]
         neg_max = [sb.tile([P, 1], F32, name="neg_max%d" % h) for h in range(QT)]
         expd = [sb.tile([P, PACK, P], F32, name="expd%d" % h) for h in range(QT)]
         total = [sb.tile([P, 1], F32, name="total%d" % h) for h in range(QT)]
         inv_total = [sb.tile([P, 1], F32, name="inv_total%d" % h) for h in range(QT)]
         excess = [sb.tile([P, PACK, P], F32, name="excess%d" % h) for h in range(QT)]
-        w_bf = [sb.tile([P, P, PACK], BF16, name="w_bf%d" % h, align_bytes=64) for h in range(QT)]
+        w_bf = [sb.tile([P, P, PACK], BF16, name="w_bf%d" % h, tag="w_bf%d" % h, align_bytes=64) for h in range(QT)]
         w_codes = [sb.tile([P, P], U32, name="w_codes%d" % h, align_bytes=64) for h in range(QT)]
         w_scales = [sb.tile([P, P], U8, name="w_scales%d" % h, align_bytes=64) for h in range(QT)]
 
         def median(h):
             x, y, z = picked[h]
-            lo = sb.tile([P, I], F32, name="lo%d" % h)
+            lo = sb.tile([P, I], F32, name="lo%d" % h, tag="lo%d" % h)
             hi = sb.tile([P, I], F32, name="hi%d" % h)
             nc.vector.tensor_tensor(out=hi[:], in0=x[:], in1=y[:], op=ALU.max)
             nc.vector.tensor_tensor(out=lo[:], in0=x[:], in1=y[:], op=ALU.min)
@@ -182,24 +177,42 @@ def tile_attend_middle_excess_blend_pl_kernel(
             )
 
         v_picked = [sb.tile([P, I], BF16, name="v_picked%d" % j) for j in range(PACK)]
-        v_bf = [sb.tile([P, 2 * P * PACK], BF16, name="v_bf%d" % g, align_bytes=64) for g in range(2)]
         v_codes = [sb.tile([P, 2 * P], U32, name="v_codes%d" % g, align_bytes=64) for g in range(2)]
         v_scales = [sb.tile([P, 2 * P], U8, name="v_scales%d" % g, align_bytes=64) for g in range(2)]
 
+        v_turned = []
+
         def values(g):
-            turned = bank(6 + (g + 1) % 2, "v_turned%d" % g)
+            turned = bank(6 + g, "v_turned%d" % g)
+            v_turned.append(turned)
             for jj in range(2):
                 j = 2 * g + jj
-                gather(j in (0, 3), v_picked[j][:], vals_sb[j][:], 0)
+                gather(j == 0, v_picked[j][:], vals_sb[j][:], 0)
                 words = v_picked[j][:].bitcast(F32)
                 for u in range(2):
                     col = (2 * jj + u) * P
                     nc.tensor.transpose(turned[:, col : col + P], words[:, u : I // 2 : 2], ident[:])
+
+        def quantise_values(g):
+            v_bf = sb.tile([P, 2 * P * PACK], BF16, name="v_bf%d" % g, tag="neg_s%d" % g, align_bytes=64)
             nc.scalar.copy(
-                out=v_bf[g][:].bitcast(F32).rearrange("p (j e u) -> p j e u", j=2, u=2),
-                in_=turned[:].rearrange("p (j u e) -> p j e u", j=2, u=2),
+                out=v_bf[:].bitcast(F32).rearrange("p (j e u) -> p j e u", j=2, u=2),
+                in_=v_turned[g][:].rearrange("p (j u e) -> p j e u", j=2, u=2),
             )
-            nc.vector.quantize_mx(out=v_codes[g][:].bitcast(FP8X4), scales=v_scales[g][:], in_=v_bf[g][:])
+            nc.vector.quantize_mx(out=v_codes[g][:].bitcast(FP8X4), scales=v_scales[g][:], in_=v_bf[:])
+
+        def keep(h):
+            if h == 0:
+                kept = sb.tile([P, PACK, P], F32, name="kept0", tag="lo0")
+            else:
+                kept = sb.tile([P, PACK, P], F32, name="kept1", tag="w_bf0", align_bytes=64)
+            nc.vector.tensor_tensor(
+                out=kept[:],
+                in0=before_sb[:, :, h * P : (h + 1) * P],
+                in1=hold_ps[:, h * P : (h + 1) * P].unsqueeze(1).to_broadcast([P, PACK, P]),
+                op=ALU.mult,
+            )
+            return kept
 
         y_sb = [sb.tile([P, PACK, P], F32, name="y_sb%d" % h) for h in range(QT)]
         y_bf = [sb.tile([P, P, PACK], BF16, name="y_bf%d" % h, align_bytes=64) for h in range(QT)]
@@ -208,7 +221,7 @@ def tile_attend_middle_excess_blend_pl_kernel(
         out_rows = out_0.rearrange("(p j) q -> p j q", j=PACK)
         out_words = out_1[0].rearrange("p q t -> p (q t)").bitcast(I32)
 
-        def blend(h):
+        def blend(h, kept):
             cols = slice(h * P, (h + 1) * P)
             acc = bank(4 + h, "o%d" % h)
             for j in range(PACK):
@@ -229,7 +242,7 @@ def tile_attend_middle_excess_blend_pl_kernel(
                 in1=rest_row[:, cols].unsqueeze(1).to_broadcast([P, PACK, P]),
                 op=ALU.mult,
             )
-            nc.vector.tensor_tensor(out=y_sb[h][:], in0=fresh[:], in1=kept[:, :, cols], op=ALU.add)
+            nc.vector.tensor_tensor(out=y_sb[h][:], in0=fresh[:], in1=kept[:], op=ALU.add)
             nc.sync.dma_start(out=out_rows[:, :, cols], in_=y_sb[h][:])
             if h == 0:
                 nc.scalar.copy(out=y_bf[h][:], in_=y_sb[h][:].rearrange("p j q -> p q j"))
@@ -240,21 +253,22 @@ def tile_attend_middle_excess_blend_pl_kernel(
             )
             nc.sync.dma_start(out=out_words[:, cols], in_=y_codes[h][:].bitcast(I32))
 
-        gather(True, picked[0][0][:], a_sb[0][:], 0)
-        gather(False, picked[0][2][:], a_sb[0][:], 2)
-        gather(True, picked[0][1][:], a_sb[0][:], 1)
+        for h in range(QT):
+            for k in range(3):
+                gather(k == 0, picked[h][k][:], a_sb[h][:], k)
         median(0)
-        for k in range(3):
-            gather(False, picked[1][k][:], a_sb[1][:], k)
-        exponent(0)
         median(1)
-        weights(0)
         values(0)
-        exponent(1)
         values(1)
+        exponent(0)
+        exponent(1)
+        quantise_values(0)
+        quantise_values(1)
+        weights(0)
         weights(1)
-        blend(0)
-        blend(1)
+        kept_tiles = [keep(0), keep(1)]
+        blend(0, kept_tiles[0])
+        blend(1, kept_tiles[1])
         for quad in range(4):
             queue = nc.scalar if quad % 2 else nc.sync
             queue.dma_start(

from contextlib import ExitStack

import concourse.mybir as mybir
from concourse.masks import make_identity

D, T, I, Q, E = 512, 2048, 512, 256, 512
FLOPS = 2 * D * Q * T + 2 * I * E * Q

F32 = mybir.dt.float32
BF16 = mybir.dt.bfloat16
I32 = mybir.dt.int32
U32 = mybir.dt.uint32
U16 = mybir.dt.uint16
U8 = mybir.dt.uint8
FP8X4 = mybir.dt.float8_e4m3fn_x4
FP4X4 = mybir.dt.float4_e2m1fn_x4
ALU = mybir.AluOpType
ACT = mybir.ActivationFunctionType

P = 128
PACK = 4
BANK = 512
QT = Q // P


def tile_attend_middle_excess_blend_pl_kernel(
    tc, query, keys_words, keys_scales, lam, level, slot_factor, vals, before, hold, offs, offs2, offs3,
    out_0, out_1, out_2,
):
    nc = tc.nc
    with ExitStack() as ctx:
        sb = ctx.enter_context(tc.tile_pool(name="sb", bufs=1))
        ps = ctx.enter_context(tc.psum_pool(name="ps", bufs=1))

        def bank(b, name):
            return ps.tile([P, BANK], F32, name=name, tag="bank%d" % b)

        key_scales = sb.tile([P, T], U8, name="key_scales", align_bytes=64)
        nc.vector.memset(key_scales[:].bitcast(I32), 0)

        query_rows = query.rearrange("(p t) q -> p t q", t=PACK)
        q_raw = [sb.tile([P, PACK, P], F32, name="q_raw%d" % h) for h in range(QT)]
        key_words = [sb.tile([P, T], U8, name="key_words%d" % c, align_bytes=64) for c in range(2)]
        before_sb = sb.tile([P, PACK, Q], F32, name="before_sb")
        lists = [sb.tile([P, I // 16], U16, name="list%d" % k) for k in range(3)]
        vals_rows = vals.rearrange("(p j) t -> j p t", j=PACK)
        vals_sb = [sb.tile([P, T], F32, name="vals_sb%d" % j) for j in range(PACK)]
        factor_col = sb.tile([P, PACK], F32, name="factor_col")
        hold_col = sb.tile([P, QT], F32, name="hold_col")
        lam_col = sb.tile([P, QT], F32, name="lam_col")
        level_col = sb.tile([P, QT], F32, name="level_col")
        ident = sb.tile([P, P], F32, name="ident")

        def load_keys(c):
            nc.sync.dma_start(
                out=key_words[c][:].bitcast(I32), in_=keys_words[0, :, c * T : (c + 1) * T].bitcast(I32)
            )

        def load_columns(dst, src):
            with nc.allow_non_contiguous_dma(reason="one value a partition"):
                nc.sync.dma_start(out=dst, in_=src)

        nc.sync.dma_start(out=q_raw[0][:], in_=query_rows[:, :, 0:P])
        load_keys(0)
        for quad in range(4):
            nc.sync.dma_start(
                out=key_scales[32 * quad : 32 * quad + 4, :].bitcast(I32),
                in_=keys_scales[0, 4 * quad : 4 * quad + 4, :].bitcast(I32),
            )
        nc.sync.dma_start(out=q_raw[1][:], in_=query_rows[:, :, P : 2 * P])
        load_keys(1)
        for k, src in enumerate((offs, offs2, offs3)):
            nc.sync.dma_start(lists[k][:], src)
        load_columns(hold_col[:], hold.rearrange("o (h p) -> p (o h)", p=P))
        nc.sync.dma_start(out=before_sb[:], in_=before.rearrange("(p j) q -> p j q", j=PACK))
        for j in range(PACK):
            nc.sync.dma_start(out=vals_sb[j][:], in_=vals_rows[j])
        load_columns(lam_col[:], lam.rearrange("(h p) o -> p (h o)", p=P))
        load_columns(level_col[:], level.rearrange("(h p) o -> p (h o)", p=P))
        nc.sync.dma_start(out=factor_col[:], in_=slot_factor.rearrange("o (p t) -> p (o t)", t=PACK))
        make_identity(nc, ident[:])

        q_bf = [sb.tile([P, P, PACK], BF16, name="q_bf%d" % h, align_bytes=64) for h in range(QT)]
        q_codes = [sb.tile([P, P], U32, name="q_codes%d" % h, align_bytes=64) for h in range(QT)]
        q_scales = [sb.tile([P, P], U8, name="q_scales%d" % h, align_bytes=64) for h in range(QT)]
        a_sb = [sb.tile([P, T], F32, name="a_sb%d" % h) for h in range(QT)]
        score_banks = [[0, 1, 2, 3], [4, 5, 0, 1]]
        for h in range(QT):
            nc.vector.tensor_copy(out=q_bf[h][:], in_=q_raw[h][:].rearrange("p t q -> p q t"))
            nc.vector.quantize_mx(
                out=q_codes[h][:].bitcast(FP8X4), scales=q_scales[h][:], in_=q_bf[h][:].rearrange("p q t -> p (q t)")
            )
        for h in range(QT):
            for c in range(T // BANK):
                acc = bank(score_banks[h][c], "score%d_%d" % (h, c))
                half, rest = divmod(c, 2)
                nc.tensor.matmul_mx(
                    out=acc[:],
                    lhsT=q_codes[h][:].bitcast(FP8X4),
                    lhsT_scale=q_scales[h][:],
                    rhs=key_words[half][:, rest * 2 * BANK : (rest + 1) * 2 * BANK].bitcast(FP4X4),
                    rhs_scale=key_scales[:, c * BANK : (c + 1) * BANK],
                    start=True,
                    stop=True,
                )
                dst = a_sb[h][:, c * BANK : (c + 1) * BANK]
                if c % 2 == 1:
                    nc.vector.tensor_copy(out=dst, in_=acc[:])
                else:
                    nc.scalar.copy(out=dst, in_=acc[:])

        hold_ps = bank(0, "hold_ps")
        for h in range(QT):
            nc.tensor.transpose(hold_ps[:, h * P : (h + 1) * P], hold_col[:, h : h + 1].to_broadcast([P, P]), ident[:])
        rest_row = sb.tile([P, Q], F32, name="rest_row")
        nc.scalar.activation(out=rest_row[:], in_=hold_ps[:, 0:Q], func=ACT.Copy, scale=-1.0, bias=1.0)
        neg_lam = sb.tile([P, QT], F32, name="neg_lam")
        nc.gpsimd.tensor_scalar(neg_lam[:], lam_col[:], -1.0, 0.0, op0=ALU.mult, op1=ALU.add)

        def gather(on_vector, dst, window, k):
            if on_vector:
                nc.vector.tensor_copy(dst, window.indirect(lists[k][:]))
            else:
                nc.scalar.activation(dst, window.indirect(lists[k][:]), ACT.Copy)

        picked = [[sb.tile([P, I], F32, name="picked%d_%d" % (h, k)) for k in range(3)] for h in range(QT)]
        neg_s = [sb.tile([P, I], F32, name="neg_s%d" % h, tag="neg_s%d" % h, align_bytes=64) for h in range(QT)]
        neg_max = [sb.tile([P, 1], F32, name="neg_max%d" % h) for h in range(QT)]
        expd = [sb.tile([P, PACK, P], F32, name="expd%d" % h) for h in range(QT)]
        total = [sb.tile([P, 1], F32, name="total%d" % h) for h in range(QT)]
        inv_total = [sb.tile([P, 1], F32, name="inv_total%d" % h) for h in range(QT)]
        excess = [sb.tile([P, PACK, P], F32, name="excess%d" % h) for h in range(QT)]
        w_bf = [sb.tile([P, P, PACK], BF16, name="w_bf%d" % h, tag="w_bf%d" % h, align_bytes=64) for h in range(QT)]
        w_codes = [sb.tile([P, P], U32, name="w_codes%d" % h, align_bytes=64) for h in range(QT)]
        w_scales = [sb.tile([P, P], U8, name="w_scales%d" % h, align_bytes=64) for h in range(QT)]

        def median(h):
            x, y, z = picked[h]
            lo = sb.tile([P, I], F32, name="lo%d" % h, tag="lo%d" % h)
            hi = sb.tile([P, I], F32, name="hi%d" % h)
            nc.vector.tensor_tensor(out=hi[:], in0=x[:], in1=y[:], op=ALU.max)
            nc.vector.tensor_tensor(out=lo[:], in0=x[:], in1=y[:], op=ALU.min)
            nc.vector.tensor_tensor(out=hi[:], in0=hi[:], in1=z[:], op=ALU.min)
            nc.vector.tensor_tensor(out=lo[:], in0=lo[:], in1=hi[:], op=ALU.max)
            nc.vector.tensor_scalar(
                neg_s[h][:], lo[:], neg_lam[:, h : h + 1], None, op0=ALU.mult, op1=ALU.min, accum_out=neg_max[h][:]
            )

        def exponent(h):
            nc.scalar.activation(
                out=expd[h][:].rearrange("p t s -> p s t"),
                in_=neg_s[h][:].rearrange("p (s t) -> p s t", t=PACK),
                func=ACT.Exp,
                bias=neg_max[h][:],
                scale=-1.0,
                accum_out=total[h][:],
            )

        def weights(h):
            nc.vector.reciprocal(inv_total[h][:], total[h][:])
            nc.vector.tensor_scalar(
                excess[h][:], expd[h][:], level_col[:, h : h + 1], inv_total[h][:], op0=ALU.subtract, op1=ALU.mult
            )
            turned = bank(2 + h, "w_turned%d" % h)
            for t in range(PACK):
                nc.tensor.transpose(turned[:, t * P : (t + 1) * P], excess[h][:, t, :], ident[:])
            nc.vector.scalar_tensor_tensor(
                out=w_bf[h][:],
                in0=turned[:].rearrange("p (t q) -> p q t", t=PACK),
                scalar=0.0,
                in1=factor_col[:].unsqueeze(1).to_broadcast([P, P, PACK]),
                op0=ALU.max,
                op1=ALU.mult,
            )
            nc.vector.quantize_mx(
                out=w_codes[h][:].bitcast(FP8X4), scales=w_scales[h][:], in_=w_bf[h][:].rearrange("p q t -> p (q t)")
            )

        v_picked = [sb.tile([P, I], BF16, name="v_picked%d" % j) for j in range(PACK)]
        v_codes = [sb.tile([P, 2 * P], U32, name="v_codes%d" % g, align_bytes=64) for g in range(2)]
        v_scales = [sb.tile([P, 2 * P], U8, name="v_scales%d" % g, align_bytes=64) for g in range(2)]

        v_turned = []

        def values(g):
            turned = bank(6 + g, "v_turned%d" % g)
            v_turned.append(turned)
            for jj in range(2):
                j = 2 * g + jj
                gather(j == 0, v_picked[j][:], vals_sb[j][:], 0)
                words = v_picked[j][:].bitcast(F32)
                for u in range(2):
                    col = (2 * jj + u) * P
                    nc.tensor.transpose(turned[:, col : col + P], words[:, u : I // 2 : 2], ident[:])

        def quantise_values(g):
            v_bf = sb.tile([P, 2 * P * PACK], BF16, name="v_bf%d" % g, tag="neg_s%d" % g, align_bytes=64)
            nc.scalar.copy(
                out=v_bf[:].bitcast(F32).rearrange("p (j e u) -> p j e u", j=2, u=2),
                in_=v_turned[g][:].rearrange("p (j u e) -> p j e u", j=2, u=2),
            )
            nc.vector.quantize_mx(out=v_codes[g][:].bitcast(FP8X4), scales=v_scales[g][:], in_=v_bf[:])

        def keep(h):
            if h == 0:
                kept = sb.tile([P, PACK, P], F32, name="kept0", tag="lo0")
            else:
                kept = sb.tile([P, PACK, P], F32, name="kept1", tag="w_bf0", align_bytes=64)
            nc.vector.tensor_tensor(
                out=kept[:],
                in0=before_sb[:, :, h * P : (h + 1) * P],
                in1=hold_ps[:, h * P : (h + 1) * P].unsqueeze(1).to_broadcast([P, PACK, P]),
                op=ALU.mult,
            )
            return kept

        y_sb = [sb.tile([P, PACK, P], F32, name="y_sb%d" % h) for h in range(QT)]
        y_bf = [sb.tile([P, P, PACK], BF16, name="y_bf%d" % h, align_bytes=64) for h in range(QT)]
        y_codes = [sb.tile([P, P], U32, name="y_codes%d" % h, align_bytes=64) for h in range(QT)]
        y_scales = sb.tile([P, Q], U8, name="y_scales", align_bytes=64)
        out_rows = out_0.rearrange("(p j) q -> p j q", j=PACK)
        out_words = out_1[0].rearrange("p q t -> p (q t)").bitcast(I32)

        def blend(h, kept):
            cols = slice(h * P, (h + 1) * P)
            acc = bank(4 + h, "o%d" % h)
            for j in range(PACK):
                g, jj = divmod(j, 2)
                nc.tensor.matmul_mx(
                    out=acc[:, j * P : (j + 1) * P],
                    lhsT=v_codes[g][:, jj * P : (jj + 1) * P].bitcast(FP8X4),
                    lhsT_scale=v_scales[g][:, jj * P : (jj + 1) * P],
                    rhs=w_codes[h][:].bitcast(FP8X4),
                    rhs_scale=w_scales[h][:],
                    start=True,
                    stop=True,
                )
            fresh = sb.tile([P, PACK, P], F32, name="fresh%d" % h)
            nc.vector.tensor_tensor(
                out=fresh[:],
                in0=acc[:].rearrange("p (j q) -> p j q", j=PACK),
                in1=rest_row[:, cols].unsqueeze(1).to_broadcast([P, PACK, P]),
                op=ALU.mult,
            )
            nc.vector.tensor_tensor(out=y_sb[h][:], in0=fresh[:], in1=kept[:], op=ALU.add)
            nc.sync.dma_start(out=out_rows[:, :, cols], in_=y_sb[h][:])
            if h == 0:
                nc.scalar.copy(out=y_bf[h][:], in_=y_sb[h][:].rearrange("p j q -> p q j"))
            else:
                nc.vector.tensor_copy(out=y_bf[h][:], in_=y_sb[h][:].rearrange("p j q -> p q j"))
            nc.vector.quantize_mx(
                out=y_codes[h][:].bitcast(FP8X4), scales=y_scales[:, cols], in_=y_bf[h][:].rearrange("p q t -> p (q t)")
            )
            nc.sync.dma_start(out=out_words[:, cols], in_=y_codes[h][:].bitcast(I32))

        for h in range(QT):
            for k in range(3):
                gather(k == 0, picked[h][k][:], a_sb[h][:], k)
        median(0)
        median(1)
        values(0)
        values(1)
        exponent(0)
        exponent(1)
        quantise_values(0)
        quantise_values(1)
        weights(0)
        weights(1)
        kept_tiles = [keep(0), keep(1)]
        blend(0, kept_tiles[0])
        blend(1, kept_tiles[1])
        for quad in range(4):
            queue = nc.scalar if quad % 2 else nc.sync
            queue.dma_start(
                out=out_2[0, 4 * quad : 4 * quad + 4, :].bitcast(I32),
                in_=y_scales[32 * quad : 32 * quad + 4, :].bitcast(I32),
            )
